import numpy as np
import ml_dtypes


def mxq(x, axis, fmt="e4m3"):
    dtype, down = {"e4m3": (ml_dtypes.float8_e4m3fn, 7), "e5m2": (ml_dtypes.float8_e5m2, 14)}[fmt]
    v = np.moveaxis(np.asarray(x, np.float32).astype(ml_dtypes.bfloat16).astype(np.float64), axis, -1)
    blocks = v.reshape(v.shape[:-1] + (-1, 32))
    amax = np.abs(blocks).max(-1, keepdims=True)
    byte = np.maximum(np.where(amax > 0, np.frexp(amax)[1] - 1 + 127, 0) - down, 1)
    scale = np.exp2(byte - 127.0)
    codes = (blocks / scale).astype(np.float32).astype(dtype).astype(np.float64)
    return np.moveaxis((codes * scale).reshape(v.shape), -1, axis)


WIDE = False


def mx_kscale(k):
    if not WIDE:
        return np.ones(k)
    levels = np.array([10, -10, 5, -5, 0])
    if k % 512:
        return np.exp2(np.random.permutation(np.resize(levels, k // 32))).repeat(32)
    a = np.empty((k // 512, 16))
    for p in range(k // 512):
        a[p, :8] = np.random.permutation(np.resize(levels, 8))
        for g in range(8):
            far = levels[np.abs(levels - a[p, g]) >= 10]
            a[p, g + 8] = far[np.random.randint(len(far))]
    return np.exp2(a.ravel()).repeat(32)


def f64(x):
    return np.asarray(x).astype(np.float64)


def striped(idx):
    return np.tile(idx.reshape(-1, 16).T, (8, 1)).astype(np.uint16)


def unstriped(offs):
    return offs[:16].T.reshape(-1).astype(np.int64)


def pack_weight(w):
    k, n = w.shape
    w = f64(np.asarray(w, np.float32).astype(ml_dtypes.bfloat16)).reshape(k // 32, 32, n)
    amax = np.abs(w).max(1)
    byte = np.clip(np.where(amax > 0, np.frexp(amax)[1] - 1 + 127 - 7, 1), 1, 254)
    scaled = (w * np.exp2(127.0 - byte)[:, None, :]).reshape(k, n).astype(np.float32)
    words = np.ascontiguousarray(scaled.reshape(k // 512, 128, 4, n).transpose(0, 1, 3, 2)).astype(ml_dtypes.float8_e4m3fn).view(np.uint8)
    return words, np.ascontiguousarray(byte.astype(np.uint8).reshape(k // 512, 16, n))


def unpack_weight(words, scales):
    g, p, n, _ = words.shape
    vals = np.ascontiguousarray(words).view(ml_dtypes.float8_e4m3fn).astype(np.float64) * np.repeat(np.exp2(scales.astype(np.float64) - 127.0), 8, axis=1)[..., None]
    return vals.transpose(0, 1, 3, 2).reshape(g * 512, n)


def sigmoid(v):
    return 1.0 / (1.0 + np.exp(-np.maximum(v, -700.0)))


K, T, S, V, H, W, G = 512, 1024, 512, 512, 512, 1024, 2048
P = 2 ** 7


def setup_inputs():
    n = np.random.standard_normal
    s = mx_kscale(K)[:, None]
    u = mx_kscale(H)
    packed_xT = pack_weight(n((K, T)) * s)
    packed_eT = pack_weight(n((K, W)) * s)
    packed_vT = pack_weight(n((H, G)) / np.sqrt(H) / u[:, None])
    return {
        "x_words": packed_xT[0],
        "x_scales": packed_xT[1],
        "e_words": packed_eT[0],
        "e_scales": packed_eT[1],
        "w1": (n((K, H)) / np.sqrt(K) / s * u).astype(np.float32),
        "w2": (n((K, H)) / np.sqrt(K) / s).astype(np.float32),
        "v_words": packed_vT[0],
        "v_scales": packed_vT[1],
        "bias": (np.tile(0.5 * np.random.standard_normal(G), (P, 1))).astype(np.float32),
        "offs": striped(np.random.permutation(T)[:S]),
        "rel": striped(np.random.permutation(W)[:S]),
        "tail": striped(np.random.permutation(G)[:V]),
    }


def reference(x_words, x_scales, e_words, e_scales, w1, w2, v_words, v_scales, bias, offs, rel, tail):
    xq = unpack_weight(x_words, x_scales)[:, unstriped(offs)]
    y = mxq(f64(w1), 0, "e4m3").T @ xq
    e_rel = unpack_weight(e_words, e_scales)[:, unstriped(rel)]
    r = sigmoid(mxq(f64(w2), 0, "e4m3").T @ e_rel)
    z = y * r
    v_tail = unpack_weight(v_words, v_scales)[:, unstriped(tail)]
    return sigmoid((mxq(z, 0, "e4m3").T @ v_tail) + f64(bias)[:1][:, unstriped(tail)])

@@ -1,0 +1,193 @@
+from contextlib import ExitStack
+
+import concourse.mybir as mybir
+from concourse.masks import make_identity
+
+F32 = mybir.dt.float32
+BF16 = mybir.dt.bfloat16
+I32 = mybir.dt.int32
+U32 = mybir.dt.uint32
+U16 = mybir.dt.uint16
+U8 = mybir.dt.uint8
+FP8X4 = mybir.dt.float8_e4m3fn_x4
+SIGMOID = mybir.ActivationFunctionType.Sigmoid
+MULT = mybir.AluOpType.mult
+ADD = mybir.AluOpType.add
+
+P = 128
+PACK = 4
+N = 512
+BLOCKS = N // P
+HALVES = 2
+POOL_BLOCKS = 0
+
+FLOPS = 3 * 2 * 512 * 512 * 512
+
+
+def tile_picked_zkge_sigmoid_p_kernel(
+    tc, x_words, x_scales, e_words, e_scales, w1, w2, v_words, v_scales, bias, offs, rel, tail, out
+):
+    nc = tc.nc
+    with ExitStack() as ctx:
+        lists = ctx.enter_context(tc.tile_pool(name="lists", bufs=1))
+        keep = ctx.enter_context(tc.tile_pool(name="keep", bufs=1))
+        psum = ctx.enter_context(tc.psum_pool(name="psum", bufs=1))
+
+        def sb(shape, dtype, name, tag=""):
+            return keep.tile(shape, dtype, name=name, tag=tag or name, align_bytes=64)
+
+        def load_list(src, name):
+            tile = lists.tile([P, N // 16], U16, name=name)
+            nc.sync.dma_start(tile[:], src)
+            return tile
+
+        def zeroed_plane(engine, width, name):
+            plane = sb([P, width], U8, name)
+            engine.memset(plane[:].bitcast(I32), 0)
+            return plane
+
+        def load_plane(queue, plane, scales):
+            for r in range(4):
+                queue.dma_start(plane[r:P:32, :].bitcast(I32), scales[0, r:16:4, :].bitcast(I32))
+
+        def load_words(words, name):
+            tile = sb([P, words.shape[2]], U32, name)
+            nc.sync.dma_start(tile[:].bitcast(I32), words[0].rearrange("p n t -> p (n t)").bitcast(I32))
+            return tile
+
+        def load_weight(w, h, name):
+            width = N // HALVES
+            raw = sb([P, PACK, width], F32, name + "_raw%d" % h)
+            nc.sync.dma_start(raw[:], w.rearrange("(p j) c -> p j c", j=PACK)[:, :, h * width : (h + 1) * width])
+            return raw
+
+        def gather(window, offsets, dtype, name):
+            picked = sb([P, 16 * offsets.shape[1]], dtype, name)
+            nc.vector.tensor_copy(picked[:], window[:].indirect(offsets))
+            return picked
+
+        def round_weight(halves, name):
+            grouped = sb([P, PACK * N], BF16, name)
+            view = grouped[:].rearrange("p (t m j) -> p m j t", t=PACK, j=PACK)
+            rows = P // HALVES
+            for h, raw in enumerate(halves):
+                nc.scalar.copy(view[:, h * rows : (h + 1) * rows], raw[:].rearrange("p j (m t) -> p m j t", t=PACK))
+            return grouped
+
+        def quantize(values, width, name, tag=""):
+            codes = sb([P, width], U32, name + "_codes", tag)
+            plane = sb([P, width], U8, name + "_plane")
+            nc.vector.quantize_mx(out=codes[:].bitcast(FP8X4), scales=plane[:], in_=values[:])
+            return codes, plane
+
+        def project(weight, codes, plane, tag):
+            bank = psum.tile([P, PACK, P], F32, name=tag + "_bank", tag=tag)
+            for t in range(PACK):
+                rows = slice(t * P, (t + 1) * P)
+                nc.tensor.matmul_mx(
+                    out=bank[:, t, :],
+                    lhsT=weight[0][:, rows].bitcast(FP8X4),
+                    lhsT_scale=weight[1][:, rows],
+                    rhs=codes.bitcast(FP8X4),
+                    rhs_scale=plane,
+                    start=True,
+                    stop=True,
+                )
+            return bank
+
+        warm_in = sb([P, 1], F32, "warm_in")
+        warm_out = sb([P, 1], F32, "warm_out")
+        nc.gpsimd.memset(warm_in[:], 0.0)
+        nc.scalar.activation(warm_out[:], warm_in[:], SIGMOID)
+
+        e_plane = zeroed_plane(nc.vector, e_scales.shape[2], "e_plane")
+        x_plane = zeroed_plane(nc.vector, x_scales.shape[2], "x_plane")
+        v_plane = zeroed_plane(nc.gpsimd, v_scales.shape[2], "v_plane")
+        bias_table = sb([P, bias.shape[1]], F32, "bias_table")
+        for q in range(4):
+            nc.vector.memset(bias_table[:, q * N : (q + 1) * N], 0.0)
+        load_plane(nc.gpsimd, v_plane, v_scales)
+        identity = sb([P, P], F32, "identity")
+        make_identity(nc, identity[:])
+
+        rel_list = load_list(rel, "rel_list")
+        e_table = load_words(e_words, "e_table")
+        load_plane(nc.sync, e_plane, e_scales)
+        w2_raw = [load_weight(w2, h, "w2") for h in range(HALVES)]
+        offs_list = load_list(offs, "offs_list")
+        load_plane(nc.sync, x_plane, x_scales)
+        x_table = load_words(x_words, "x_table")
+        w1_raw = [load_weight(w1, 0, "w1")]
+        tail_list = load_list(tail, "tail_list")
+        nc.sync.dma_start(bias_table[0:1, :], bias[0:1, :])
+        w1_raw.append(load_weight(w1, 1, "w1"))
+        v_table = load_words(v_words, "v_table")
+
+        e_codes = gather(e_table, rel_list[:], U32, "e_codes")
+        e_bytes = gather(e_plane, rel_list[:], U8, "e_bytes")
+        x_bytes = gather(x_plane, offs_list[:], U8, "x_bytes")
+        x_codes = gather(x_table, offs_list[:], U32, "x_codes")
+        w2_q = quantize(round_weight(w2_raw, "w2_bf"), N, "w2", "x_table")
+        v_bytes = gather(v_plane, tail_list[:], U8, "v_bytes")
+        bias_row = gather(bias_table, tail_list[:], F32, "bias_row")
+        w1_q = quantize(round_weight(w1_raw, "w1_bf"), N, "w1")
+        v_codes = gather(v_table, tail_list[:], U32, "v_codes")
+
+        gates = sb([P, BLOCKS, P, PACK], F32, "gates", "w1_raw1")
+
+        def gate(b):
+            cols = slice(b * P, (b + 1) * P)
+            bank = project(w2_q, e_codes[:, cols], e_bytes[:, cols], "r%d" % b)
+            nc.scalar.activation(gates[:, b], bank[:].rearrange("p t n -> p n t"), SIGMOID)
+
+        gate(0)
+        gate(1)
+        turned = psum.tile([P, BLOCKS, P], F32, name="bias_turned", tag="r0")
+        for b in range(BLOCKS):
+            nc.tensor.transpose(turned[:, b, :], bias_row[:, b * P : (b + 1) * P], identity[:])
+        bias_col = sb([P, BLOCKS], F32, "bias_col")
+        nc.scalar.copy(bias_col[:], turned[:, :, 0])
+        spread = psum.tile([P, N], F32, name="bias_spread", tag="r0")
+        for b in range(BLOCKS):
+            nc.tensor.transpose(spread[:, b * P : (b + 1) * P], bias_col[:, b : b + 1].to_broadcast([P, P]), identity[:])
+        bias_picked = sb([P, N], F32, "bias_picked")
+        nc.scalar.copy(bias_picked[:], spread[:])
+        gate(2)
+        gate(3)
+
+        heads = []
+        for b in range(BLOCKS):
+            cols = slice(b * P, (b + 1) * P)
+            heads.append(project(w1_q, x_codes[:, cols], x_bytes[:, cols], "y%d" % b))
+
+        z_bf = sb([P, BLOCKS, P * PACK], BF16, "z_bf", "v_table")
+        z_q = []
+        for b in range(BLOCKS + 1):
+            if b < BLOCKS:
+                nc.vector.tensor_tensor(
+                    z_bf[:, b].rearrange("p (n t) -> p n t", t=PACK), heads[b][:].rearrange("p t n -> p n t"), gates[:, b], MULT
+                )
+            if b > 0:
+                z_q.append(quantize(z_bf[:, b - 1], P, "z%d" % (b - 1)))
+
+        for b in range(BLOCKS):
+            bank = psum.tile([P, N], F32, name="score_bank%d" % b, tag="r%d" % b)
+            nc.tensor.matmul_mx(
+                out=bank[:],
+                lhsT=z_q[b][0][:].bitcast(FP8X4),
+                lhsT_scale=z_q[b][1][:],
+                rhs=v_codes[:].bitcast(FP8X4),
+                rhs_scale=v_bytes[:],
+                start=True,
+                stop=True,
+            )
+            logits = sb([P, N], F32, "logits%d" % b)
+            if b < POOL_BLOCKS:
+                sums = sb([P, N], F32, "sums%d" % b)
+                nc.scalar.copy(sums[:], bank[:])
+                nc.gpsimd.tensor_tensor(logits[:], sums[:], bias_picked[:], ADD)
+            else:
+                nc.vector.tensor_tensor(logits[:], bank[:], bias_picked[:], ADD)
+            scores = sb([P, N], F32, "scores%d" % b)
+            nc.scalar.activation(scores[:], logits[:], SIGMOID)
+            nc.sync.dma_start(out[b * P : (b + 1) * P, :], scores[:])

@@ -55,10 +55,9 @@ def tile_picked_zkge_sigmoid_p_kernel(
             nc.sync.dma_start(tile[:].bitcast(I32), words[0].rearrange("p n t -> p (n t)").bitcast(I32))
             return tile
 
-        def load_weight(w, h, name):
-            width = N // HALVES
-            raw = sb([P, PACK, width], F32, name + "_raw%d" % h)
-            nc.sync.dma_start(raw[:], w.rearrange("(p j) c -> p j c", j=PACK)[:, :, h * width : (h + 1) * width])
+        def load_weight(w, name):
+            raw = sb([P, PACK, N], F32, name)
+            nc.sync.dma_start(raw[:], w.rearrange("(p j) c -> p j c", j=PACK))
             return raw
 
         def gather(window, offsets, dtype, name):
@@ -66,18 +65,22 @@ def tile_picked_zkge_sigmoid_p_kernel(
             nc.vector.tensor_copy(picked[:], window[:].indirect(offsets))
             return picked
 
-        def round_weight(halves, name):
-            grouped = sb([P, PACK * N], BF16, name)
-            view = grouped[:].rearrange("p (t m j) -> p m j t", t=PACK, j=PACK)
-            rows = P // HALVES
-            for h, raw in enumerate(halves):
-                nc.scalar.copy(view[:, h * rows : (h + 1) * rows], raw[:].rearrange("p j (m t) -> p m j t", t=PACK))
-            return grouped
+        def round_weight(raw, name):
+            pairs = []
+            columns = raw[:].rearrange("p j (m u i) -> p u m j i", u=2, i=2)
+            for u in range(2):
+                grouped = sb([P, 2 * N], BF16, name + "%d" % u)
+                nc.scalar.copy(grouped[:].rearrange("p (i m j) -> p m j i", i=2, j=PACK), columns[:, u])
+                pairs.append(grouped)
+            return pairs
 
-        def quantize(values, width, name, tag=""):
+        def quantize(pieces, width, name, tag=""):
             codes = sb([P, width], U32, name + "_codes", tag)
             plane = sb([P, width], U8, name + "_plane")
-            nc.vector.quantize_mx(out=codes[:].bitcast(FP8X4), scales=plane[:], in_=values[:])
+            step = width // len(pieces)
+            for i, values in enumerate(pieces):
+                cols = slice(i * step, (i + 1) * step)
+                nc.vector.quantize_mx(out=codes[:, cols].bitcast(FP8X4), scales=plane[:, cols], in_=values[:])
             return codes, plane
 
         def project(weight, codes, plane, tag):
@@ -102,43 +105,44 @@ def tile_picked_zkge_sigmoid_p_kernel(
 
         e_plane = zeroed_plane(nc.vector, e_scales.shape[2], "e_plane")
         x_plane = zeroed_plane(nc.vector, x_scales.shape[2], "x_plane")
-        v_plane = zeroed_plane(nc.gpsimd, v_scales.shape[2], "v_plane")
+        v_plane = zeroed_plane(nc.vector, v_scales.shape[2], "v_plane")
         bias_table = sb([P, bias.shape[1]], F32, "bias_table")
-        for q in range(4):
-            nc.vector.memset(bias_table[:, q * N : (q + 1) * N], 0.0)
-        load_plane(nc.gpsimd, v_plane, v_scales)
+        nc.vector.memset(bias_table[:].bitcast(I32), 0)
         identity = sb([P, P], F32, "identity")
         make_identity(nc, identity[:])
 
         rel_list = load_list(rel, "rel_list")
         e_table = load_words(e_words, "e_table")
         load_plane(nc.sync, e_plane, e_scales)
-        w2_raw = [load_weight(w2, h, "w2") for h in range(HALVES)]
         offs_list = load_list(offs, "offs_list")
-        load_plane(nc.sync, x_plane, x_scales)
         x_table = load_words(x_words, "x_table")
-        w1_raw = [load_weight(w1, 0, "w1")]
+        w2_raw = load_weight(w2, "w2_raw")
+        load_plane(nc.sync, x_plane, x_scales)
         tail_list = load_list(tail, "tail_list")
         nc.sync.dma_start(bias_table[0:1, :], bias[0:1, :])
-        w1_raw.append(load_weight(w1, 1, "w1"))
+        w1_raw = load_weight(w1, "w1_raw")
+        load_plane(nc.sync, v_plane, v_scales)
         v_table = load_words(v_words, "v_table")
 
         e_codes = gather(e_table, rel_list[:], U32, "e_codes")
         e_bytes = gather(e_plane, rel_list[:], U8, "e_bytes")
-        x_bytes = gather(x_plane, offs_list[:], U8, "x_bytes")
         x_codes = gather(x_table, offs_list[:], U32, "x_codes")
-        w2_q = quantize(round_weight(w2_raw, "w2_bf"), N, "w2", "x_table")
-        v_bytes = gather(v_plane, tail_list[:], U8, "v_bytes")
+        x_bytes = gather(x_plane, offs_list[:], U8, "x_bytes")
         bias_row = gather(bias_table, tail_list[:], F32, "bias_row")
-        w1_q = quantize(round_weight(w1_raw, "w1_bf"), N, "w1")
+        w2_q = quantize(round_weight(w2_raw, "w2_bf"), N, "w2", "bias_table")
+        v_bytes = gather(v_plane, tail_list[:], U8, "v_bytes")
+        w1_q = quantize(round_weight(w1_raw, "w1_bf"), N, "w1", "v_plane")
         v_codes = gather(v_table, tail_list[:], U32, "v_codes")
 
-        gates = sb([P, BLOCKS, P, PACK], F32, "gates", "w1_raw1")
+        def in_pairs(bank):
+            return bank[:].rearrange("p t (n i) -> p n t i", i=2)
+
+        gates = sb([P, BLOCKS, P // 2, PACK, 2], F32, "gates", "w1_raw")
 
         def gate(b):
             cols = slice(b * P, (b + 1) * P)
             bank = project(w2_q, e_codes[:, cols], e_bytes[:, cols], "r%d" % b)
-            nc.scalar.activation(gates[:, b], bank[:].rearrange("p t n -> p n t"), SIGMOID)
+            nc.scalar.activation(gates[:, b], in_pairs(bank), SIGMOID)
 
         gate(0)
         gate(1)
@@ -164,30 +168,30 @@ def tile_picked_zkge_sigmoid_p_kernel(
         z_q = []
         for b in range(BLOCKS + 1):
             if b < BLOCKS:
-                nc.vector.tensor_tensor(
-                    z_bf[:, b].rearrange("p (n t) -> p n t", t=PACK), heads[b][:].rearrange("p t n -> p n t"), gates[:, b], MULT
-                )
+                z_view = z_bf[:, b].rearrange("p (n i t) -> p n t i", i=2, t=PACK)
+                nc.vector.tensor_tensor(z_view, in_pairs(heads[b]), gates[:, b], MULT)
             if b > 0:
-                z_q.append(quantize(z_bf[:, b - 1], P, "z%d" % (b - 1)))
+                z_q.append(quantize([z_bf[:, b - 1]], P, "z%d" % (b - 1)))
 
-        for b in range(BLOCKS):
-            bank = psum.tile([P, N], F32, name="score_bank%d" % b, tag="r%d" % b)
+        pieces = [(b, 0, N) for b in range(BLOCKS - 1)] + [(BLOCKS - 1, 0, N // 2), (BLOCKS - 1, N // 2, N)]
+        for i, (b, lo, hi) in enumerate(pieces):
+            bank = psum.tile([P, hi - lo], F32, name="score_bank%d" % i, tag="r%d" % i if i < BLOCKS else "y0")
             nc.tensor.matmul_mx(
                 out=bank[:],
                 lhsT=z_q[b][0][:].bitcast(FP8X4),
                 lhsT_scale=z_q[b][1][:],
-                rhs=v_codes[:].bitcast(FP8X4),
-                rhs_scale=v_bytes[:],
+                rhs=v_codes[:, lo:hi].bitcast(FP8X4),
+                rhs_scale=v_bytes[:, lo:hi],
                 start=True,
                 stop=True,
             )
-            logits = sb([P, N], F32, "logits%d" % b)
+            logits = sb([P, hi - lo], F32, "logits%d" % i)
             if b < POOL_BLOCKS:
                 sums = sb([P, N], F32, "sums%d" % b)
                 nc.scalar.copy(sums[:], bank[:])
                 nc.gpsimd.tensor_tensor(logits[:], sums[:], bias_picked[:], ADD)
             else:
-                nc.vector.tensor_tensor(logits[:], bank[:], bias_picked[:], ADD)
-            scores = sb([P, N], F32, "scores%d" % b)
+                nc.vector.tensor_tensor(logits[:], bank[:], bias_picked[:, lo:hi], ADD)
+            scores = sb([P, hi - lo], F32, "scores%d" % i)
             nc.scalar.activation(scores[:], logits[:], SIGMOID)
-            nc.sync.dma_start(out[b * P : (b + 1) * P, :], scores[:])
+            nc.sync.dma_start(out[b * P : (b + 1) * P, lo:hi], scores[:])

from contextlib import ExitStack

import concourse.mybir as mybir
from concourse.masks import make_identity

F32 = mybir.dt.float32
BF16 = mybir.dt.bfloat16
I32 = mybir.dt.int32
U32 = mybir.dt.uint32
U16 = mybir.dt.uint16
U8 = mybir.dt.uint8
FP8X4 = mybir.dt.float8_e4m3fn_x4
SIGMOID = mybir.ActivationFunctionType.Sigmoid
MULT = mybir.AluOpType.mult
ADD = mybir.AluOpType.add

P = 128
PACK = 4
N = 512
BLOCKS = N // P
HALVES = 2
POOL_BLOCKS = 0

FLOPS = 3 * 2 * 512 * 512 * 512


def tile_picked_zkge_sigmoid_p_kernel(
    tc, x_words, x_scales, e_words, e_scales, w1, w2, v_words, v_scales, bias, offs, rel, tail, out
):
    nc = tc.nc
    with ExitStack() as ctx:
        lists = ctx.enter_context(tc.tile_pool(name="lists", bufs=1))
        keep = ctx.enter_context(tc.tile_pool(name="keep", bufs=1))
        psum = ctx.enter_context(tc.psum_pool(name="psum", bufs=1))

        def sb(shape, dtype, name, tag=""):
            return keep.tile(shape, dtype, name=name, tag=tag or name, align_bytes=64)

        def load_list(src, name):
            tile = lists.tile([P, N // 16], U16, name=name)
            nc.sync.dma_start(tile[:], src)
            return tile

        def zeroed_plane(engine, width, name):
            plane = sb([P, width], U8, name)
            engine.memset(plane[:].bitcast(I32), 0)
            return plane

        def load_plane(queue, plane, scales):
            for r in range(4):
                queue.dma_start(plane[r:P:32, :].bitcast(I32), scales[0, r:16:4, :].bitcast(I32))

        def load_words(words, name):
            tile = sb([P, words.shape[2]], U32, name)
            nc.sync.dma_start(tile[:].bitcast(I32), words[0].rearrange("p n t -> p (n t)").bitcast(I32))
            return tile

        def load_weight(w, name):
            raw = sb([P, PACK, N], F32, name)
            nc.sync.dma_start(raw[:], w.rearrange("(p j) c -> p j c", j=PACK))
            return raw

        def gather(window, offsets, dtype, name):
            picked = sb([P, 16 * offsets.shape[1]], dtype, name)
            nc.vector.tensor_copy(picked[:], window[:].indirect(offsets))
            return picked

        def round_weight(raw, name):
            pairs = []
            columns = raw[:].rearrange("p j (m u i) -> p u m j i", u=2, i=2)
            for u in range(2):
                grouped = sb([P, 2 * N], BF16, name + "%d" % u)
                nc.scalar.copy(grouped[:].rearrange("p (i m j) -> p m j i", i=2, j=PACK), columns[:, u])
                pairs.append(grouped)
            return pairs

        def quantize(pieces, width, name, tag=""):
            codes = sb([P, width], U32, name + "_codes", tag)
            plane = sb([P, width], U8, name + "_plane")
            step = width // len(pieces)
            for i, values in enumerate(pieces):
                cols = slice(i * step, (i + 1) * step)
                nc.vector.quantize_mx(out=codes[:, cols].bitcast(FP8X4), scales=plane[:, cols], in_=values[:])
            return codes, plane

        def project(weight, codes, plane, tag):
            bank = psum.tile([P, PACK, P], F32, name=tag + "_bank", tag=tag)
            for t in range(PACK):
                rows = slice(t * P, (t + 1) * P)
                nc.tensor.matmul_mx(
                    out=bank[:, t, :],
                    lhsT=weight[0][:, rows].bitcast(FP8X4),
                    lhsT_scale=weight[1][:, rows],
                    rhs=codes.bitcast(FP8X4),
                    rhs_scale=plane,
                    start=True,
                    stop=True,
                )
            return bank

        warm_in = sb([P, 1], F32, "warm_in")
        warm_out = sb([P, 1], F32, "warm_out")
        nc.gpsimd.memset(warm_in[:], 0.0)
        nc.scalar.activation(warm_out[:], warm_in[:], SIGMOID)

        e_plane = zeroed_plane(nc.vector, e_scales.shape[2], "e_plane")
        x_plane = zeroed_plane(nc.vector, x_scales.shape[2], "x_plane")
        v_plane = zeroed_plane(nc.vector, v_scales.shape[2], "v_plane")
        bias_table = sb([P, bias.shape[1]], F32, "bias_table")
        nc.vector.memset(bias_table[:].bitcast(I32), 0)
        identity = sb([P, P], F32, "identity")
        make_identity(nc, identity[:])

        rel_list = load_list(rel, "rel_list")
        e_table = load_words(e_words, "e_table")
        load_plane(nc.sync, e_plane, e_scales)
        offs_list = load_list(offs, "offs_list")
        x_table = load_words(x_words, "x_table")
        w2_raw = load_weight(w2, "w2_raw")
        load_plane(nc.sync, x_plane, x_scales)
        tail_list = load_list(tail, "tail_list")
        nc.sync.dma_start(bias_table[0:1, :], bias[0:1, :])
        w1_raw = load_weight(w1, "w1_raw")
        load_plane(nc.sync, v_plane, v_scales)
        v_table = load_words(v_words, "v_table")

        e_codes = gather(e_table, rel_list[:], U32, "e_codes")
        e_bytes = gather(e_plane, rel_list[:], U8, "e_bytes")
        x_codes = gather(x_table, offs_list[:], U32, "x_codes")
        x_bytes = gather(x_plane, offs_list[:], U8, "x_bytes")
        bias_row = gather(bias_table, tail_list[:], F32, "bias_row")
        w2_q = quantize(round_weight(w2_raw, "w2_bf"), N, "w2", "bias_table")
        v_bytes = gather(v_plane, tail_list[:], U8, "v_bytes")
        w1_q = quantize(round_weight(w1_raw, "w1_bf"), N, "w1", "v_plane")
        v_codes = gather(v_table, tail_list[:], U32, "v_codes")

        def in_pairs(bank):
            return bank[:].rearrange("p t (n i) -> p n t i", i=2)

        gates = sb([P, BLOCKS, P // 2, PACK, 2], F32, "gates", "w1_raw")

        def gate(b):
            cols = slice(b * P, (b + 1) * P)
            bank = project(w2_q, e_codes[:, cols], e_bytes[:, cols], "r%d" % b)
            nc.scalar.activation(gates[:, b], in_pairs(bank), SIGMOID)

        gate(0)
        gate(1)
        turned = psum.tile([P, BLOCKS, P], F32, name="bias_turned", tag="r0")
        for b in range(BLOCKS):
            nc.tensor.transpose(turned[:, b, :], bias_row[:, b * P : (b + 1) * P], identity[:])
        bias_col = sb([P, BLOCKS], F32, "bias_col")
        nc.scalar.copy(bias_col[:], turned[:, :, 0])
        spread = psum.tile([P, N], F32, name="bias_spread", tag="r0")
        for b in range(BLOCKS):
            nc.tensor.transpose(spread[:, b * P : (b + 1) * P], bias_col[:, b : b + 1].to_broadcast([P, P]), identity[:])
        bias_picked = sb([P, N], F32, "bias_picked")
        nc.scalar.copy(bias_picked[:], spread[:])
        gate(2)
        gate(3)

        heads = []
        for b in range(BLOCKS):
            cols = slice(b * P, (b + 1) * P)
            heads.append(project(w1_q, x_codes[:, cols], x_bytes[:, cols], "y%d" % b))

        z_bf = sb([P, BLOCKS, P * PACK], BF16, "z_bf", "v_table")
        z_q = []
        for b in range(BLOCKS + 1):
            if b < BLOCKS:
                z_view = z_bf[:, b].rearrange("p (n i t) -> p n t i", i=2, t=PACK)
                nc.vector.tensor_tensor(z_view, in_pairs(heads[b]), gates[:, b], MULT)
            if b > 0:
                z_q.append(quantize([z_bf[:, b - 1]], P, "z%d" % (b - 1)))

        pieces = [(b, 0, N) for b in range(BLOCKS - 1)] + [(BLOCKS - 1, 0, N // 2), (BLOCKS - 1, N // 2, N)]
        for i, (b, lo, hi) in enumerate(pieces):
            bank = psum.tile([P, hi - lo], F32, name="score_bank%d" % i, tag="r%d" % i if i < BLOCKS else "y0")
            nc.tensor.matmul_mx(
                out=bank[:],
                lhsT=z_q[b][0][:].bitcast(FP8X4),
                lhsT_scale=z_q[b][1][:],
                rhs=v_codes[:, lo:hi].bitcast(FP8X4),
                rhs_scale=v_bytes[:, lo:hi],
                start=True,
                stop=True,
            )
            logits = sb([P, hi - lo], F32, "logits%d" % i)
            if b < POOL_BLOCKS:
                sums = sb([P, N], F32, "sums%d" % b)
                nc.scalar.copy(sums[:], bank[:])
                nc.gpsimd.tensor_tensor(logits[:], sums[:], bias_picked[:], ADD)
            else:
                nc.vector.tensor_tensor(logits[:], bank[:], bias_picked[:, lo:hi], ADD)
            scores = sb([P, hi - lo], F32, "scores%d" % i)
            nc.scalar.activation(scores[:], logits[:], SIGMOID)
            nc.sync.dma_start(out[b * P : (b + 1) * P, lo:hi], scores[:])
